import numpy as np, ml_dtypes
CORES = [120,124,248,252,376,380,504,508]
N = 8
import mx_ref
NC, D = 256, 5
SRC = [[0,4,5,6,7],[2,3,4,5,6],[1,3,4,5,6],[0,2,4,5,6],[0,1,2,4,5],[0,3,4,6,7],[0,1,2,4,6],[1,3,4,5,7]]
BF = ml_dtypes.bfloat16
def setup_inputs(rng):
    def f(*shape):
        return mx_ref.flush((rng.standard_normal(shape, dtype=np.float32) * np.exp2(rng.integers(-2, 3, shape[:-1] + (1,)))).astype(BF))
    return {"w": f(N, 128, D * 512), "x": f(N, 128, 4 * NC)}
def setup_inputs_blocks(rng):
    d = setup_inputs(rng)
    for k in ("w", "x"): d[k] = mx_ref.spread(d[k], rng, 2)
    return d
def setup_inputs_wide(rng):
    d = setup_inputs(rng)
    for k in ("w", "x"): d[k] = mx_ref.flush((d[k].astype(np.float32) * np.exp2(rng.integers(-8, 9, (N, 1, 1))).astype(np.float32)).astype(BF))
    return d
def setup_inputs_zeros(rng):
    d = setup_inputs(rng); v = d["x"].reshape(N, 128, -1, 4).copy()
    v[np.broadcast_to((rng.random((N, 1, v.shape[2], 1)) < 0.33), v.shape)] = 0
    d["x"] = v.reshape(d["x"].shape)
    return d
def reference(w, x):
    QX = [mx_ref.quantize(x[j]) for j in range(N)]
    y = np.zeros((N, 128, NC), np.float32)
    for r in range(N):
        for i in range(D):
            p = mx_ref.matmul(mx_ref.quantize(w[r][:, 512 * i:512 * i + 512]), QX[SRC[r][i]])
            y[r] = p if i == 0 else y[r] + p
    return {"y": y}

@@ -1,0 +1,191 @@
+from concourse.bass import DstId, RemoteDMATransfer
+from concourse.mybir import dt
+
+NCOL = 256
+WCOL = 128
+D = 5
+N = 8
+
+SCRATCH = {
+    "xb": ("sbuf", [128, 4 * NCOL], "bfloat16"),
+    "wb": ("sbuf", [128, 4 * WCOL * D], "bfloat16"),
+    "wq": ("sbuf", [128, WCOL * D], "float8_e4m3fn_x4"),
+    "ws": ("sbuf", [128, WCOL * D], "uint8"),
+    "q": ("sbuf", [128, NCOL * (D + 1)], "float8_e4m3fn_x4"),
+    "s": ("sbuf", [128, NCOL * (D + 1)], "uint8"),
+    "acc": ("psum", [128, 512], "float32"),
+    "yb": ("sbuf", [128, NCOL], "float32"),
+}
+SEMAPHORES = ["xin", "win", "xq", "wqd", "sent", "mm", "out", "done"] + ["a%d" % j for j in range(N)]
+
+_PLANS = {}
+
+
+def _bits(mask):
+    return [b for b in range(mask.bit_length()) if (mask >> b) & 1]
+
+
+def _mask(bits):
+    m = 0
+    for b in bits:
+        m |= 1 << b
+    return m
+
+
+def _plan(cores, src, topo):
+    if "p" in _PLANS:
+        return _PLANS["p"]
+    n = len(cores)
+
+    def way(a, b):
+        a, b = cores[a], cores[b]
+        if not topo.may_write(a, b):
+            return None
+        if topo.host(a) == topo.host(b) and topo.chip(a) == topo.chip(b):
+            return "chip"
+        return "switch" if topo.same_plane(a, b) else "cable"
+
+    def same_die(a, b):
+        return topo.die(cores[a]) == topo.die(cores[b])
+
+    first = [[] for _ in range(n)]
+    beside = [[] for _ in range(n)]
+    choices = []
+    for j in range(n):
+        hosts = {}
+        for r in range(n):
+            if r != j and j in src[r]:
+                hosts.setdefault(topo.host(cores[r]), []).append(r)
+        got, far = [], []
+        for rs in hosts.values():
+            k = way(j, rs[0])
+            if k == "chip":
+                beside[j] += [(j, r) for r in rs]
+            elif k is None:
+                far += rs
+            else:
+                p = ([r for r in rs if same_die(j, r)] or rs)[0]
+                first[j].append((j, p))
+                got.append(p)
+                choices += [[(j, p, r), (j, j, r)] for r in rs if r != p]
+        choices += [[(j, h, r) for h in got if way(h, r)] for r in far]
+
+    best = [None, None]
+
+    def search(i, load, picked):
+        if i == len(choices):
+            crowded = sum(1 for r in range(n) if not beside[r] and sum(load.get((r, k), 0) for k in ("chip", "switch", "cable")) > 2)
+            off = [(s, d) for (_, s, d) in picked if way(s, d) != "chip"]
+            cost = (crowded, len(off), sum(1 for (s, d) in off if not same_die(s, d)))
+            if best[0] is None or cost < best[0]:
+                best[0], best[1] = cost, list(picked)
+            return
+        for (j, s, d) in choices[i]:
+            key = (s, way(s, d))
+            if load.get(key, 0) == 0:
+                load[key] = 1
+                picked.append((j, s, d))
+                search(i + 1, load, picked)
+                picked.pop()
+                load[key] = 0
+
+    search(0, {}, [])
+    again = [[(j, d) for (j, s, d) in best[1] if s == r and j == r] for r in range(n)]
+    onward = [[(j, d) for (j, s, d) in best[1] if s == r and j != r] for r in range(n)]
+
+    groups = [[] for _ in range(n)]
+    due = [{} for _ in range(n)]
+
+    def emit(r, writes, stage, upper_ok):
+        off = [(j, d) for (j, d) in writes if way(r, d) != "chip"]
+        on = [(j, d) for (j, d) in writes if way(r, d) == "chip"]
+        grp = []
+        for (j, d) in off:
+            low = _bits(topo.mask(cores[r], cores[d]))
+            eng = low if len(off) == 1 else (low[0::2] if way(r, d) == "switch" else low[1::2])
+            grp.append((j, d, eng, stage))
+        tail = []
+        for (j, d) in on:
+            far_mask = 0
+            for o in range(n):
+                if way(r, o) not in (None, "chip"):
+                    far_mask |= topo.mask(cores[r], cores[o])
+            eng = _bits(topo.mask(cores[r], cores[d]) & ~far_mask)
+            (grp if upper_ok or not off else tail).append((j, d, eng, stage + 1 if off and not upper_ok else stage))
+        for part in (grp, tail):
+            if part:
+                groups[r].append([(j, d, e) for (j, d, e, _) in part])
+                for (j, d, e, st) in part:
+                    due[d][j] = (st, 2 * len(e))
+
+    for r in range(n):
+        emit(r, first[r], 2, True)
+        emit(r, beside[r] + again[r], 3, True)
+    for r in range(n):
+        emit(r, onward[r], 4, bool(beside[r]))
+    _PLANS["p"] = (groups, due)
+    return _PLANS["p"]
+
+
+def rank_program(g, core, T, topo):
+    rank = T.rank_of(core)
+    if rank is None:
+        return
+    src = T.tables["SRC"]
+    groups, due = _plan(T.cores, src, topo)
+    S = T.sem
+
+    def cols(r, j):
+        a = NCOL * (src[r].index(j) if j in src[r] else D)
+        return a, a + NCOL
+
+    g.sync.dma_start(T.xb[:], T.x[:]).then_inc(S.xin, 16)
+    g.sync.dma_start(T.wb[:], T.w[:]).then_inc(S.win, 16)
+
+    a, b = cols(rank, rank)
+    g.vector.wait_ge(S.xin, 16)
+    g.vector.quantize_mx(T.q[:, a:b], T.s[:, a:b], T.xb[:]).then_inc(S.xq, 1)
+    g.vector.wait_ge(S.win, 16)
+    for i in range(D):
+        g.vector.quantize_mx(T.wq[:, WCOL * i:WCOL * (i + 1)], T.ws[:, WCOL * i:WCOL * (i + 1)],
+                             T.wb[:, 4 * WCOL * i:4 * WCOL * (i + 1)]).then_inc(S.wqd, 1)
+
+    left = 0
+    g.wait_ge(S.xq, 1)
+    for grp in groups[rank]:
+        for j in sorted({j for (j, _, _) in grp if j != rank}):
+            g.wait_ge(S["a%d" % j], due[rank][j][1])
+        for codes in (True, False):
+            buf = T.q if codes else T.s
+            trs = []
+            for (j, d, eng) in grp:
+                sa, sb = cols(rank, j)
+                da, db = cols(d, j)
+                rid, pid = topo.addr(T.cores[d], core)
+                s_ap, d_ap = buf[:, sa:sb], buf[:, da:db]
+                if codes:
+                    s_ap, d_ap = s_ap.bitcast(dt.uint8), d_ap.bitcast(dt.uint8)
+                trs.append(RemoteDMATransfer(dst_ids=[DstId(rid=rid, pnc=pid)], dma_engine_mask=_mask(eng),
+                                             remote_sem=S["a%d" % j], src=s_ap, dst=d_ap))
+                left += len(eng)
+            g.remote_dma_fused(trs, local_sem=S.sent)
+
+    order = sorted(src[rank], key=lambda j: (0, j) if j == rank else (due[rank][j][0], j))
+    g.tensor.wait_ge(S.wqd, D)
+    for k, j in enumerate(order):
+        if j == rank:
+            g.tensor.wait_ge(S.xq, 1)
+        else:
+            g.tensor.wait_ge(S["a%d" % j], due[rank][j][1])
+        i = src[rank].index(j)
+        a, b = cols(rank, j)
+        mm = g.tensor.matmul_mx(T.acc[:, 0:NCOL], T.wq[:, WCOL * i:WCOL * (i + 1)], T.ws[:, WCOL * i:WCOL * (i + 1)],
+                                T.q[:, a:b], T.s[:, a:b], k == 0, k == D - 1)
+    mm.then_inc(S.mm, 1)
+
+    g.vector.wait_ge(S.mm, 1)
+    g.vector.tensor_copy(T.yb[:], T.acc[:, 0:NCOL]).then_inc(S.out, 1)
+    g.sync.wait_ge(S.out, 1)
+    g.sync.dma_start(T.y[:], T.yb[:]).then_inc(S.done, 16)
+    g.sync.wait_ge(S.done, 16)
+    g.wait_ge(S.sent, left)

@@ -2,7 +2,9 @@ from concourse.bass import DstId, RemoteDMATransfer
 from concourse.mybir import dt
 
 NCOL = 256
+HCOL = 128
 WCOL = 128
+BANK = 512
 D = 5
 N = 8
 
@@ -13,10 +15,11 @@ SCRATCH = {
     "ws": ("sbuf", [128, WCOL * D], "uint8"),
     "q": ("sbuf", [128, NCOL * (D + 1)], "float8_e4m3fn_x4"),
     "s": ("sbuf", [128, NCOL * (D + 1)], "uint8"),
-    "acc": ("psum", [128, 512], "float32"),
+    "acc": ("psum", [128, 2 * BANK], "float32"),
     "yb": ("sbuf", [128, NCOL], "float32"),
 }
-SEMAPHORES = ["xin", "win", "xq", "wqd", "sent", "mm", "out", "done"] + ["a%d" % j for j in range(N)]
+SEMAPHORES = (["xin0", "xin1", "win", "xq0", "xq1", "wqd", "sent", "mm0", "mm1", "out0", "out1", "done"]
+              + ["a%d_%d" % (j, p) for j in range(N) for p in range(2)])
 
 _PLANS = {}
 
@@ -96,33 +99,47 @@ def _plan(cores, src, topo):
     groups = [[] for _ in range(n)]
     due = [{} for _ in range(n)]
 
-    def emit(r, writes, stage, upper_ok):
-        off = [(j, d) for (j, d) in writes if way(r, d) != "chip"]
-        on = [(j, d) for (j, d) in writes if way(r, d) == "chip"]
-        grp = []
-        for (j, d) in off:
-            low = _bits(topo.mask(cores[r], cores[d]))
-            eng = low if len(off) == 1 else (low[0::2] if way(r, d) == "switch" else low[1::2])
-            grp.append((j, d, eng, stage))
-        tail = []
-        for (j, d) in on:
-            far_mask = 0
-            for o in range(n):
-                if way(r, o) not in (None, "chip"):
-                    far_mask |= topo.mask(cores[r], cores[o])
-            eng = _bits(topo.mask(cores[r], cores[d]) & ~far_mask)
-            (grp if upper_ok or not off else tail).append((j, d, eng, stage + 1 if off and not upper_ok else stage))
-        for part in (grp, tail):
-            if part:
-                groups[r].append([(j, d, e) for (j, d, e, _) in part])
-                for (j, d, e, st) in part:
-                    due[d][j] = (st, 2 * len(e))
+    def engines(r, writes):
+        off = [d for (_, d) in writes if way(r, d) != "chip"]
+        far_mask = 0
+        for o in range(n):
+            if way(r, o) not in (None, "chip"):
+                far_mask |= topo.mask(cores[r], cores[o])
+        out = []
+        for (j, d) in writes:
+            m = topo.mask(cores[r], cores[d])
+            if way(r, d) == "chip":
+                out.append((j, d, _bits(m & ~far_mask)))
+            elif len(off) == 1:
+                out.append((j, d, _bits(m)))
+            else:
+                out.append((j, d, _bits(m)[0::2] if way(r, d) == "switch" else _bits(m)[1::2]))
+        return out
+
+    def add(r, grp, stage):
+        if grp:
+            groups[r].append(grp)
+            for (j, p, d, e) in grp:
+                due[d][j, p] = (stage, 2 * len(e))
+
+    def in_turn(r, writes, stage):
+        for p in range(2):
+            add(r, [(j, p, d, e) for (j, d, e) in engines(r, writes)], stage + p)
+
+    def together(r, writes, stage):
+        add(r, [(j, p, d, e[p * len(e) // 2:(p + 1) * len(e) // 2]) for (j, d, e) in engines(r, writes) for p in range(2)], stage)
 
     for r in range(n):
-        emit(r, first[r], 2, True)
-        emit(r, beside[r] + again[r], 3, True)
+        in_turn(r, first[r], 2)
+        together(r, beside[r] + again[r], 3.5)
     for r in range(n):
-        emit(r, onward[r], 4, bool(beside[r]))
+        off = [(j, d) for (j, d) in onward[r] if way(r, d) != "chip"]
+        on = [(j, d) for (j, d) in onward[r] if way(r, d) == "chip"]
+        if beside[r] or not off:
+            in_turn(r, off + on, 4)
+        else:
+            in_turn(r, off, 4)
+            together(r, on, 6)
     _PLANS["p"] = (groups, due)
     return _PLANS["p"]
 
@@ -135,57 +152,70 @@ def rank_program(g, core, T, topo):
     groups, due = _plan(T.cores, src, topo)
     S = T.sem
 
-    def cols(r, j):
-        a = NCOL * (src[r].index(j) if j in src[r] else D)
-        return a, a + NCOL
+    def cols(r, j, p):
+        a = NCOL * (src[r].index(j) if j in src[r] else D) + HCOL * p
+        return a, a + HCOL
 
-    g.sync.dma_start(T.xb[:], T.x[:]).then_inc(S.xin, 16)
+    for p in range(2):
+        g.sync.dma_start(T.xb[:, 4 * HCOL * p:4 * HCOL * (p + 1)], T.x[:, 4 * HCOL * p:4 * HCOL * (p + 1)]).then_inc(S["xin%d" % p], 16)
     g.sync.dma_start(T.wb[:], T.w[:]).then_inc(S.win, 16)
 
-    a, b = cols(rank, rank)
-    g.vector.wait_ge(S.xin, 16)
-    g.vector.quantize_mx(T.q[:, a:b], T.s[:, a:b], T.xb[:]).then_inc(S.xq, 1)
+    for p in range(2):
+        a, b = cols(rank, rank, p)
+        g.vector.wait_ge(S["xin%d" % p], 16)
+        g.vector.quantize_mx(T.q[:, a:b], T.s[:, a:b], T.xb[:, 4 * HCOL * p:4 * HCOL * (p + 1)]).then_inc(S["xq%d" % p], 1)
     g.vector.wait_ge(S.win, 16)
     for i in range(D):
         g.vector.quantize_mx(T.wq[:, WCOL * i:WCOL * (i + 1)], T.ws[:, WCOL * i:WCOL * (i + 1)],
                              T.wb[:, 4 * WCOL * i:4 * WCOL * (i + 1)]).then_inc(S.wqd, 1)
 
     left = 0
-    g.wait_ge(S.xq, 1)
     for grp in groups[rank]:
-        for j in sorted({j for (j, _, _) in grp if j != rank}):
-            g.wait_ge(S["a%d" % j], due[rank][j][1])
+        for (j, p) in sorted({(j, p) for (j, p, _, _) in grp}):
+            if j == rank:
+                g.wait_ge(S["xq%d" % p], 1)
+            else:
+                g.wait_ge(S["a%d_%d" % (j, p)], due[rank][j, p][1])
         for codes in (True, False):
             buf = T.q if codes else T.s
             trs = []
-            for (j, d, eng) in grp:
-                sa, sb = cols(rank, j)
-                da, db = cols(d, j)
+            for (j, p, d, eng) in grp:
+                sa, sb = cols(rank, j, p)
+                da, db = cols(d, j, p)
                 rid, pid = topo.addr(T.cores[d], core)
                 s_ap, d_ap = buf[:, sa:sb], buf[:, da:db]
                 if codes:
                     s_ap, d_ap = s_ap.bitcast(dt.uint8), d_ap.bitcast(dt.uint8)
                 trs.append(RemoteDMATransfer(dst_ids=[DstId(rid=rid, pnc=pid)], dma_engine_mask=_mask(eng),
-                                             remote_sem=S["a%d" % j], src=s_ap, dst=d_ap))
+                                             remote_sem=S["a%d_%d" % (j, p)], src=s_ap, dst=d_ap))
                 left += len(eng)
             g.remote_dma_fused(trs, local_sem=S.sent)
 
-    order = sorted(src[rank], key=lambda j: (0, j) if j == rank else (due[rank][j][0], j))
+    order = sorted(((j, p) for j in src[rank] for p in range(2)),
+                   key=lambda t: (p_key(t, rank, due), t[1], t[0]))
+    done = [0, 0]
     g.tensor.wait_ge(S.wqd, D)
-    for k, j in enumerate(order):
+    for (j, p) in order:
         if j == rank:
-            g.tensor.wait_ge(S.xq, 1)
+            g.tensor.wait_ge(S["xq%d" % p], 1)
         else:
-            g.tensor.wait_ge(S["a%d" % j], due[rank][j][1])
+            g.tensor.wait_ge(S["a%d_%d" % (j, p)], due[rank][j, p][1])
         i = src[rank].index(j)
-        a, b = cols(rank, j)
-        mm = g.tensor.matmul_mx(T.acc[:, 0:NCOL], T.wq[:, WCOL * i:WCOL * (i + 1)], T.ws[:, WCOL * i:WCOL * (i + 1)],
-                                T.q[:, a:b], T.s[:, a:b], k == 0, k == D - 1)
-    mm.then_inc(S.mm, 1)
+        a, b = cols(rank, j, p)
+        done[p] += 1
+        mm = g.tensor.matmul_mx(T.acc[:, BANK * p:BANK * p + HCOL], T.wq[:, WCOL * i:WCOL * (i + 1)], T.ws[:, WCOL * i:WCOL * (i + 1)],
+                                T.q[:, a:b], T.s[:, a:b], done[p] == 1, done[p] == D)
+        if done[p] == D:
+            mm.then_inc(S["mm%d" % p], 1)
 
-    g.vector.wait_ge(S.mm, 1)
-    g.vector.tensor_copy(T.yb[:], T.acc[:, 0:NCOL]).then_inc(S.out, 1)
-    g.sync.wait_ge(S.out, 1)
-    g.sync.dma_start(T.y[:], T.yb[:]).then_inc(S.done, 16)
-    g.sync.wait_ge(S.done, 16)
+    for p in range(2):
+        g.vector.wait_ge(S["mm%d" % p], 1)
+        g.vector.tensor_copy(T.yb[:, HCOL * p:HCOL * (p + 1)], T.acc[:, BANK * p:BANK * p + HCOL]).then_inc(S["out%d" % p], 1)
+        g.sync.wait_ge(S["out%d" % p], 1)
+        g.sync.dma_start(T.y[:, HCOL * p:HCOL * (p + 1)], T.yb[:, HCOL * p:HCOL * (p + 1)]).then_inc(S.done, 16)
+    g.sync.wait_ge(S.done, 32)
     g.wait_ge(S.sent, left)
+
+
+def p_key(t, rank, due):
+    return 0 if t[0] == rank else due[rank][t][0]

@@ -7,6 +7,9 @@ WCOL = 128
 BANK = 512
 D = 5
 N = 8
+PIECES = [(0, 128), (128, 256), (0, 256), (128, 192), (192, 224), (224, 256)]
+PLANE = 2
+TURN = [0, PLANE, 3, 4, 5]
 
 SCRATCH = {
     "xb": ("sbuf", [128, 4 * NCOL], "bfloat16"),
@@ -18,8 +21,8 @@ SCRATCH = {
     "acc": ("psum", [128, 2 * BANK], "float32"),
     "yb": ("sbuf", [128, NCOL], "float32"),
 }
-SEMAPHORES = (["xin0", "xin1", "win", "xq0", "xq1", "wqd", "sent", "mm0", "mm1", "out0", "out1", "done"]
-              + ["a%d_%d" % (j, p) for j in range(N) for p in range(2)])
+SEMAPHORES = (["xin0", "xin1", "win", "xq0", "xq1", "wqd", "sent", "mm0", "mm1", "out0", "out1", "done0", "done1"]
+              + ["a%d_%d" % (j, p) for j in range(N) for p in range(len(PIECES))])
 
 _PLANS = {}
 
@@ -53,7 +56,7 @@ def _plan(cores, src, topo):
 
     first = [[] for _ in range(n)]
     beside = [[] for _ in range(n)]
-    choices = []
+    onward = [[] for _ in range(n)]
     for j in range(n):
         hosts = {}
         for r in range(n):
@@ -70,77 +73,51 @@ def _plan(cores, src, topo):
                 p = ([r for r in rs if same_die(j, r)] or rs)[0]
                 first[j].append((j, p))
                 got.append(p)
-                choices += [[(j, p, r), (j, j, r)] for r in rs if r != p]
-        choices += [[(j, h, r) for h in got if way(h, r)] for r in far]
+                onward[p] += [(j, r) for r in rs if r != p]
+        for r in far:
+            onward[[h for h in got if way(h, r) == "switch"][0]].append((j, r))
 
-    best = [None, None]
-
-    def search(i, load, picked):
-        if i == len(choices):
-            crowded = sum(1 for r in range(n) if not beside[r] and sum(load.get((r, k), 0) for k in ("chip", "switch", "cable")) > 2)
-            off = [(s, d) for (_, s, d) in picked if way(s, d) != "chip"]
-            cost = (crowded, len(off), sum(1 for (s, d) in off if not same_die(s, d)))
-            if best[0] is None or cost < best[0]:
-                best[0], best[1] = cost, list(picked)
-            return
-        for (j, s, d) in choices[i]:
-            key = (s, way(s, d))
-            if load.get(key, 0) == 0:
-                load[key] = 1
-                picked.append((j, s, d))
-                search(i + 1, load, picked)
-                picked.pop()
-                load[key] = 0
-
-    search(0, {}, [])
-    again = [[(j, d) for (j, s, d) in best[1] if s == r and j == r] for r in range(n)]
-    onward = [[(j, d) for (j, s, d) in best[1] if s == r and j != r] for r in range(n)]
-
-    groups = [[] for _ in range(n)]
+    calls = [[] for _ in range(n)]
     due = [{} for _ in range(n)]
 
     def engines(r, writes):
-        off = [d for (_, d) in writes if way(r, d) != "chip"]
         far_mask = 0
         for o in range(n):
             if way(r, o) not in (None, "chip"):
                 far_mask |= topo.mask(cores[r], cores[o])
+        low = _bits(far_mask)
+        lows = [d for (_, d) in writes if way(r, d) != "chip"]
         out = []
         for (j, d) in writes:
-            m = topo.mask(cores[r], cores[d])
             if way(r, d) == "chip":
-                out.append((j, d, _bits(m & ~far_mask)))
-            elif len(off) == 1:
-                out.append((j, d, _bits(m)))
+                e = _bits(topo.mask(cores[r], cores[d]) & ~far_mask)[0::2]
+            elif len(lows) == 1:
+                e = low
             else:
-                out.append((j, d, _bits(m)[0::2] if way(r, d) == "switch" else _bits(m)[1::2]))
+                e = low[lows.index(d)::2]
+            out.append((j, d, e))
         return out
 
-    def add(r, grp, stage):
-        if grp:
-            groups[r].append(grp)
-            for (j, p, d, e) in grp:
-                due[d][j, p] = (stage, 2 * len(e))
+    def add(r, call, stage):
+        if call:
+            calls[r].append(call)
+            for (j, p, d, e) in call:
+                due[d].setdefault(j, {})[p] = (stage, len(e))
 
     def in_turn(r, writes, stage):
-        for p in range(2):
-            add(r, [(j, p, d, e) for (j, d, e) in engines(r, writes)], stage + p)
+        for k, p in enumerate(TURN):
+            add(r, [(j, p, d, e) for (j, d, e) in engines(r, writes)], stage + k / len(TURN))
 
     def together(r, writes, stage):
         add(r, [(j, p, d, e[p * len(e) // 2:(p + 1) * len(e) // 2]) for (j, d, e) in engines(r, writes) for p in range(2)], stage)
+        add(r, [(j, PLANE, d, e) for (j, d, e) in engines(r, writes)], stage)
 
     for r in range(n):
         in_turn(r, first[r], 2)
-        together(r, beside[r] + again[r], 3.5)
+        together(r, beside[r], 3)
     for r in range(n):
-        off = [(j, d) for (j, d) in onward[r] if way(r, d) != "chip"]
-        on = [(j, d) for (j, d) in onward[r] if way(r, d) == "chip"]
-        if beside[r] or not off:
-            in_turn(r, off + on, 4)
-        else:
-            in_turn(r, off, 4)
-            together(r, on, 6)
-    _PLANS["p"] = (groups, due)
+        in_turn(r, onward[r], 4)
+    _PLANS["p"] = (calls, due)
     return _PLANS["p"]
 
 
@@ -149,12 +126,25 @@ def rank_program(g, core, T, topo):
     if rank is None:
         return
     src = T.tables["SRC"]
-    groups, due = _plan(T.cores, src, topo)
+    calls, due = _plan(T.cores, src, topo)
     S = T.sem
 
     def cols(r, j, p):
-        a = NCOL * (src[r].index(j) if j in src[r] else D) + HCOL * p
-        return a, a + HCOL
+        a = NCOL * (src[r].index(j) if j in src[r] else D)
+        return a + PIECES[p][0], a + PIECES[p][1]
+
+    def wait_for(queue, j, p):
+        if j != rank:
+            queue.wait_ge(S["a%d_%d" % (j, p)], due[rank][j][p][1])
+        else:
+            for h in range(2):
+                if PIECES[p][0] < HCOL * (h + 1) and PIECES[p][1] > HCOL * h:
+                    queue.wait_ge(S["xq%d" % h], 1)
+
+    def parts(j, h):
+        if j == rank:
+            return [h]
+        return [p for p in sorted(due[rank][j]) if p == PLANE or (PIECES[p][0] < HCOL * (h + 1) and PIECES[p][1] > HCOL * h)]
 
     for p in range(2):
         g.sync.dma_start(T.xb[:, 4 * HCOL * p:4 * HCOL * (p + 1)], T.x[:, 4 * HCOL * p:4 * HCOL * (p + 1)]).then_inc(S["xin%d" % p], 16)
@@ -170,52 +160,44 @@ def rank_program(g, core, T, topo):
                              T.wb[:, 4 * WCOL * i:4 * WCOL * (i + 1)]).then_inc(S.wqd, 1)
 
     left = 0
-    for grp in groups[rank]:
-        for (j, p) in sorted({(j, p) for (j, p, _, _) in grp}):
-            if j == rank:
-                g.wait_ge(S["xq%d" % p], 1)
+    for call in calls[rank]:
+        for (j, p) in sorted({(j, p) for (j, p, _, _) in call}):
+            wait_for(g, j, p)
+        trs = []
+        for (j, p, d, eng) in call:
+            sa, sb = cols(rank, j, p)
+            da, db = cols(d, j, p)
+            rid, pid = topo.addr(T.cores[d], core)
+            if p == PLANE:
+                s_ap, d_ap = T.s[:, sa:sb], T.s[:, da:db]
             else:
-                g.wait_ge(S["a%d_%d" % (j, p)], due[rank][j, p][1])
-        for codes in (True, False):
-            buf = T.q if codes else T.s
-            trs = []
-            for (j, p, d, eng) in grp:
-                sa, sb = cols(rank, j, p)
-                da, db = cols(d, j, p)
-                rid, pid = topo.addr(T.cores[d], core)
-                s_ap, d_ap = buf[:, sa:sb], buf[:, da:db]
-                if codes:
-                    s_ap, d_ap = s_ap.bitcast(dt.uint8), d_ap.bitcast(dt.uint8)
-                trs.append(RemoteDMATransfer(dst_ids=[DstId(rid=rid, pnc=pid)], dma_engine_mask=_mask(eng),
-                                             remote_sem=S["a%d_%d" % (j, p)], src=s_ap, dst=d_ap))
-                left += len(eng)
-            g.remote_dma_fused(trs, local_sem=S.sent)
+                s_ap, d_ap = T.q[:, sa:sb].bitcast(dt.uint8), T.q[:, da:db].bitcast(dt.uint8)
+            trs.append(RemoteDMATransfer(dst_ids=[DstId(rid=rid, pnc=pid)], dma_engine_mask=_mask(eng),
+                                         remote_sem=S["a%d_%d" % (j, p)], src=s_ap, dst=d_ap))
+            left += len(eng)
+        g.remote_dma_fused(trs, local_sem=S.sent)
 
-    order = sorted(((j, p) for j in src[rank] for p in range(2)),
-                   key=lambda t: (p_key(t, rank, due), t[1], t[0]))
+    def when(t):
+        return 0 if t[0] == rank else max(due[rank][t[0]][p][0] for p in parts(*t))
+
+    order = sorted(((j, h) for j in src[rank] for h in range(2)), key=lambda t: (when(t), t[1], t[0]))
     done = [0, 0]
     g.tensor.wait_ge(S.wqd, D)
-    for (j, p) in order:
-        if j == rank:
-            g.tensor.wait_ge(S["xq%d" % p], 1)
-        else:
-            g.tensor.wait_ge(S["a%d_%d" % (j, p)], due[rank][j, p][1])
+    for (j, h) in order:
+        for p in parts(j, h):
+            wait_for(g.tensor, j, p)
         i = src[rank].index(j)
-        a, b = cols(rank, j, p)
-        done[p] += 1
-        mm = g.tensor.matmul_mx(T.acc[:, BANK * p:BANK * p + HCOL], T.wq[:, WCOL * i:WCOL * (i + 1)], T.ws[:, WCOL * i:WCOL * (i + 1)],
-                                T.q[:, a:b], T.s[:, a:b], done[p] == 1, done[p] == D)
-        if done[p] == D:
-            mm.then_inc(S["mm%d" % p], 1)
+        a, b = cols(rank, j, h)
+        done[h] += 1
+        mm = g.tensor.matmul_mx(T.acc[:, BANK * h:BANK * h + HCOL], T.wq[:, WCOL * i:WCOL * (i + 1)], T.ws[:, WCOL * i:WCOL * (i + 1)],
+                                T.q[:, a:b], T.s[:, a:b], done[h] == 1, done[h] == D)
+        if done[h] == D:
+            mm.then_inc(S["mm%d" % h], 1)
 
-    for p in range(2):
+    for p, queue in enumerate((g.sync, g.scalar)):
         g.vector.wait_ge(S["mm%d" % p], 1)
         g.vector.tensor_copy(T.yb[:, HCOL * p:HCOL * (p + 1)], T.acc[:, BANK * p:BANK * p + HCOL]).then_inc(S["out%d" % p], 1)
-        g.sync.wait_ge(S["out%d" % p], 1)
-        g.sync.dma_start(T.y[:, HCOL * p:HCOL * (p + 1)], T.yb[:, HCOL * p:HCOL * (p + 1)]).then_inc(S.done, 16)
-    g.sync.wait_ge(S.done, 32)
+        queue.wait_ge(S["out%d" % p], 1)
+        queue.dma_start(T.y[:, HCOL * p:HCOL * (p + 1)], T.yb[:, HCOL * p:HCOL * (p + 1)]).then_inc(S["done%d" % p], 16)
+        queue.wait_ge(S["done%d" % p], 16)
     g.wait_ge(S.sent, left)
-
-
-def p_key(t, rank, due):
-    return 0 if t[0] == rank else due[rank][t][0]

@@ -7,9 +7,12 @@ WCOL = 128
 BANK = 512
 D = 5
 N = 8
-PIECES = [(0, 128), (128, 256), (0, 256), (128, 192), (192, 224), (224, 256)]
+PIECES = [(0, 128), (128, 256), (0, 256), (128, 192), (192, 224), (224, 256), (0, 32), (32, 96), (96, 128), (32, 128)]
 PLANE = 2
-TURN = [0, PLANE, 3, 4, 5]
+OWN = [6, PLANE, 3, 4, 5]
+FEED = 9
+HELP = [7, 8]
+TURN = [6, PLANE, 3, 4, 7, 5, 8]
 
 SCRATCH = {
     "xb": ("sbuf", [128, 4 * NCOL], "bfloat16"),
@@ -44,53 +47,56 @@ def _plan(cores, src, topo):
     n = len(cores)
 
     def way(a, b):
-        a, b = cores[a], cores[b]
         if not topo.may_write(a, b):
             return None
         if topo.host(a) == topo.host(b) and topo.chip(a) == topo.chip(b):
             return "chip"
         return "switch" if topo.same_plane(a, b) else "cable"
 
-    def same_die(a, b):
-        return topo.die(cores[a]) == topo.die(cores[b])
+    def helper(c):
+        near = [k for k in range(max(0, c - 16), c + 16) if topo.host(k) == topo.host(c)]
+        mate = [k for k in near if topo.mates(c, k)][0]
+        return [k for k in near if way(c, k) == "chip" and k != c and k not in cores and topo.die(k) == topo.die(c)
+                and topo.may_write(k, mate) != topo.may_write(c, mate)][0]
 
-    first = [[] for _ in range(n)]
-    beside = [[] for _ in range(n)]
-    onward = [[] for _ in range(n)]
+    first = {c: [] for c in cores}
+    beside = {c: [] for c in cores}
+    onward = {c: [] for c in cores}
     for j in range(n):
+        o = cores[j]
         hosts = {}
         for r in range(n):
             if r != j and j in src[r]:
-                hosts.setdefault(topo.host(cores[r]), []).append(r)
+                hosts.setdefault(topo.host(cores[r]), []).append(cores[r])
         got, far = [], []
         for rs in hosts.values():
-            k = way(j, rs[0])
+            k = way(o, rs[0])
             if k == "chip":
-                beside[j] += [(j, r) for r in rs]
+                beside[o] += [(j, r) for r in rs]
             elif k is None:
                 far += rs
             else:
-                p = ([r for r in rs if same_die(j, r)] or rs)[0]
-                first[j].append((j, p))
+                p = ([r for r in rs if topo.die(r) == topo.die(o)] or rs)[0]
+                first[o].append((j, p))
                 got.append(p)
                 onward[p] += [(j, r) for r in rs if r != p]
         for r in far:
             onward[[h for h in got if way(h, r) == "switch"][0]].append((j, r))
 
-    calls = [[] for _ in range(n)]
-    due = [{} for _ in range(n)]
+    calls = {c: [] for c in cores}
+    due = {c: {} for c in cores}
 
-    def engines(r, writes):
+    def engines(c, writes):
         far_mask = 0
-        for o in range(n):
-            if way(r, o) not in (None, "chip"):
-                far_mask |= topo.mask(cores[r], cores[o])
+        for o in cores:
+            if way(c, o) not in (None, "chip"):
+                far_mask |= topo.mask(c, o)
         low = _bits(far_mask)
-        lows = [d for (_, d) in writes if way(r, d) != "chip"]
+        lows = [d for (_, d) in writes if way(c, d) != "chip"]
         out = []
         for (j, d) in writes:
-            if way(r, d) == "chip":
-                e = _bits(topo.mask(cores[r], cores[d]) & ~far_mask)[0::2]
+            if way(c, d) == "chip":
+                e = _bits(topo.mask(c, d) & ~far_mask)[0::2]
             elif len(lows) == 1:
                 e = low
             else:
@@ -98,76 +104,97 @@ def _plan(cores, src, topo):
             out.append((j, d, e))
         return out
 
-    def add(r, call, stage):
+    def add(c, call, stage):
         if call:
-            calls[r].append(call)
+            calls.setdefault(c, []).append(call)
             for (j, p, d, e) in call:
-                due[d].setdefault(j, {})[p] = (stage, len(e))
+                due.setdefault(d, {}).setdefault(j, {})[p] = (stage, len(e))
 
-    def in_turn(r, writes, stage):
+    def together(c, ws, stage):
+        add(c, [(j, p, d, e[p * len(e) // 2:(p + 1) * len(e) // 2]) for (j, d, e) in ws for p in range(2)], stage)
+        add(c, [(j, PLANE, d, e) for (j, d, e) in ws], stage)
+
+    for c in cores:
+        ws = engines(c, first[c])
+        cab = [w for w in ws if way(c, w[1]) == "cable"]
+        oth = [w for w in ws if way(c, w[1]) != "cable"]
+        h = helper(c)
+        add(c, [(j, OWN[0], d, e) for (j, d, e) in cab], 2)
+        add(c, [(j, FEED, hh, e) for (j, hh, e) in engines(c, [(j, h) for (j, _, _) in cab])], 2)
+        for k, p in enumerate(OWN[1:3]):
+            add(c, [(j, p, d, e) for (j, d, e) in cab], 2.1 + k / 10)
+        together(c, oth, 2.3)
+        for k, p in enumerate(OWN[3:]):
+            add(c, [(j, p, d, e) for (j, d, e) in cab], 2.4 + k / 5)
+        for k, p in enumerate(HELP):
+            add(h, [(j, p, d, _bits(topo.mask(h, d))[0::2]) for (j, d, _) in cab], 2.5 + k / 5)
+        together(c, engines(c, beside[c]), 3)
+    for c in cores:
+        slow = engines(c, [(j, d) for (j, d) in onward[c] if way(cores[j], c) == "cable"])
         for k, p in enumerate(TURN):
-            add(r, [(j, p, d, e) for (j, d, e) in engines(r, writes)], stage + k / len(TURN))
-
-    def together(r, writes, stage):
-        add(r, [(j, p, d, e[p * len(e) // 2:(p + 1) * len(e) // 2]) for (j, d, e) in engines(r, writes) for p in range(2)], stage)
-        add(r, [(j, PLANE, d, e) for (j, d, e) in engines(r, writes)], stage)
-
-    for r in range(n):
-        in_turn(r, first[r], 2)
-        together(r, beside[r], 3)
-    for r in range(n):
-        in_turn(r, onward[r], 4)
+            add(c, [(j, p, d, e) for (j, d, e) in slow], 4 + k / len(TURN))
+            if k == 1:
+                together(c, engines(c, [(j, d) for (j, d) in onward[c] if way(cores[j], c) != "cable"]), 4.3)
     _PLANS["p"] = (calls, due)
     return _PLANS["p"]
 
 
 def rank_program(g, core, T, topo):
-    rank = T.rank_of(core)
-    if rank is None:
-        return
     src = T.tables["SRC"]
     calls, due = _plan(T.cores, src, topo)
+    if core not in calls:
+        return
+    rank = T.rank_of(core)
     S = T.sem
 
-    def cols(r, j, p):
-        a = NCOL * (src[r].index(j) if j in src[r] else D)
+    def cols(c, j, p):
+        r = T.rank_of(c)
+        a = NCOL * (src[r].index(j) if r is not None and j in src[r] else D)
         return a + PIECES[p][0], a + PIECES[p][1]
 
+    def covers(p, h):
+        return PIECES[p][0] < HCOL * (h + 1) and PIECES[p][1] > HCOL * h
+
     def wait_for(queue, j, p):
-        if j != rank:
-            queue.wait_ge(S["a%d_%d" % (j, p)], due[rank][j][p][1])
-        else:
+        if j == rank:
             for h in range(2):
-                if PIECES[p][0] < HCOL * (h + 1) and PIECES[p][1] > HCOL * h:
+                if covers(p, h):
                     queue.wait_ge(S["xq%d" % h], 1)
+        elif p in due[core][j]:
+            queue.wait_ge(S["a%d_%d" % (j, p)], due[core][j][p][1])
+        else:
+            for k in sorted(due[core][j]):
+                if k != PLANE and PIECES[k][0] <= PIECES[p][0] and PIECES[p][1] <= PIECES[k][1]:
+                    queue.wait_ge(S["a%d_%d" % (j, k)], due[core][j][k][1])
 
     def parts(j, h):
         if j == rank:
             return [h]
-        return [p for p in sorted(due[rank][j]) if p == PLANE or (PIECES[p][0] < HCOL * (h + 1) and PIECES[p][1] > HCOL * h)]
+        return [p for p in sorted(due[core][j]) if p == PLANE or covers(p, h)]
 
-    for p in range(2):
-        g.sync.dma_start(T.xb[:, 4 * HCOL * p:4 * HCOL * (p + 1)], T.x[:, 4 * HCOL * p:4 * HCOL * (p + 1)]).then_inc(S["xin%d" % p], 16)
-    g.sync.dma_start(T.wb[:], T.w[:]).then_inc(S.win, 16)
+    if rank is not None:
+        for p in range(2):
+            g.sync.dma_start(T.xb[:, 4 * HCOL * p:4 * HCOL * (p + 1)], T.x[:, 4 * HCOL * p:4 * HCOL * (p + 1)]).then_inc(S["xin%d" % p], 16)
+        g.sync.dma_start(T.wb[:], T.w[:]).then_inc(S.win, 16)
 
-    for p in range(2):
-        a, b = cols(rank, rank, p)
-        g.vector.wait_ge(S["xin%d" % p], 16)
-        g.vector.quantize_mx(T.q[:, a:b], T.s[:, a:b], T.xb[:, 4 * HCOL * p:4 * HCOL * (p + 1)]).then_inc(S["xq%d" % p], 1)
-    g.vector.wait_ge(S.win, 16)
-    for i in range(D):
-        g.vector.quantize_mx(T.wq[:, WCOL * i:WCOL * (i + 1)], T.ws[:, WCOL * i:WCOL * (i + 1)],
-                             T.wb[:, 4 * WCOL * i:4 * WCOL * (i + 1)]).then_inc(S.wqd, 1)
+        for p in range(2):
+            a, b = cols(core, rank, p)
+            g.vector.wait_ge(S["xin%d" % p], 16)
+            g.vector.quantize_mx(T.q[:, a:b], T.s[:, a:b], T.xb[:, 4 * HCOL * p:4 * HCOL * (p + 1)]).then_inc(S["xq%d" % p], 1)
+        g.vector.wait_ge(S.win, 16)
+        for i in range(D):
+            g.vector.quantize_mx(T.wq[:, WCOL * i:WCOL * (i + 1)], T.ws[:, WCOL * i:WCOL * (i + 1)],
+                                 T.wb[:, 4 * WCOL * i:4 * WCOL * (i + 1)]).then_inc(S.wqd, 1)
 
     left = 0
-    for call in calls[rank]:
+    for call in calls[core]:
         for (j, p) in sorted({(j, p) for (j, p, _, _) in call}):
             wait_for(g, j, p)
         trs = []
         for (j, p, d, eng) in call:
-            sa, sb = cols(rank, j, p)
+            sa, sb = cols(core, j, p)
             da, db = cols(d, j, p)
-            rid, pid = topo.addr(T.cores[d], core)
+            rid, pid = topo.addr(d, core)
             if p == PLANE:
                 s_ap, d_ap = T.s[:, sa:sb], T.s[:, da:db]
             else:
@@ -177,27 +204,28 @@ def rank_program(g, core, T, topo):
             left += len(eng)
         g.remote_dma_fused(trs, local_sem=S.sent)
 
-    def when(t):
-        return 0 if t[0] == rank else max(due[rank][t[0]][p][0] for p in parts(*t))
+    if rank is not None:
+        def when(t):
+            return 0 if t[0] == rank else max(due[core][t[0]][p][0] for p in parts(*t))
 
-    order = sorted(((j, h) for j in src[rank] for h in range(2)), key=lambda t: (when(t), t[1], t[0]))
-    done = [0, 0]
-    g.tensor.wait_ge(S.wqd, D)
-    for (j, h) in order:
-        for p in parts(j, h):
-            wait_for(g.tensor, j, p)
-        i = src[rank].index(j)
-        a, b = cols(rank, j, h)
-        done[h] += 1
-        mm = g.tensor.matmul_mx(T.acc[:, BANK * h:BANK * h + HCOL], T.wq[:, WCOL * i:WCOL * (i + 1)], T.ws[:, WCOL * i:WCOL * (i + 1)],
-                                T.q[:, a:b], T.s[:, a:b], done[h] == 1, done[h] == D)
-        if done[h] == D:
-            mm.then_inc(S["mm%d" % h], 1)
+        order = sorted(((j, h) for j in src[rank] for h in range(2)), key=lambda t: (when(t), t[1], t[0]))
+        done = [0, 0]
+        g.tensor.wait_ge(S.wqd, D)
+        for (j, h) in order:
+            for p in parts(j, h):
+                wait_for(g.tensor, j, p)
+            i = src[rank].index(j)
+            a, b = cols(core, j, h)
+            done[h] += 1
+            mm = g.tensor.matmul_mx(T.acc[:, BANK * h:BANK * h + HCOL], T.wq[:, WCOL * i:WCOL * (i + 1)], T.ws[:, WCOL * i:WCOL * (i + 1)],
+                                    T.q[:, a:b], T.s[:, a:b], done[h] == 1, done[h] == D)
+            if done[h] == D:
+                mm.then_inc(S["mm%d" % h], 1)
 
-    for p, queue in enumerate((g.sync, g.scalar)):
-        g.vector.wait_ge(S["mm%d" % p], 1)
-        g.vector.tensor_copy(T.yb[:, HCOL * p:HCOL * (p + 1)], T.acc[:, BANK * p:BANK * p + HCOL]).then_inc(S["out%d" % p], 1)
-        queue.wait_ge(S["out%d" % p], 1)
-        queue.dma_start(T.y[:, HCOL * p:HCOL * (p + 1)], T.yb[:, HCOL * p:HCOL * (p + 1)]).then_inc(S["done%d" % p], 16)
-        queue.wait_ge(S["done%d" % p], 16)
+        for p, queue in enumerate((g.sync, g.scalar)):
+            g.vector.wait_ge(S["mm%d" % p], 1)
+            g.vector.tensor_copy(T.yb[:, HCOL * p:HCOL * (p + 1)], T.acc[:, BANK * p:BANK * p + HCOL]).then_inc(S["out%d" % p], 1)
+            queue.wait_ge(S["out%d" % p], 1)
+            queue.dma_start(T.y[:, HCOL * p:HCOL * (p + 1)], T.yb[:, HCOL * p:HCOL * (p + 1)]).then_inc(S["done%d" % p], 16)
+            queue.wait_ge(S["done%d" % p], 16)
     g.wait_ge(S.sent, left)

from concourse.bass import DstId, RemoteDMATransfer
from concourse.mybir import dt

NCOL = 256
HCOL = 128
WCOL = 128
BANK = 512
D = 5
N = 8
PIECES = [(0, 128), (128, 256), (0, 256), (128, 192), (192, 224), (224, 256), (0, 32), (32, 96), (96, 128), (32, 128)]
PLANE = 2
OWN = [6, PLANE, 3, 4, 5]
FEED = 9
HELP = [7, 8]
TURN = [6, PLANE, 3, 4, 7, 5, 8]

SCRATCH = {
    "xb": ("sbuf", [128, 4 * NCOL], "bfloat16"),
    "wb": ("sbuf", [128, 4 * WCOL * D], "bfloat16"),
    "wq": ("sbuf", [128, WCOL * D], "float8_e4m3fn_x4"),
    "ws": ("sbuf", [128, WCOL * D], "uint8"),
    "q": ("sbuf", [128, NCOL * (D + 1)], "float8_e4m3fn_x4"),
    "s": ("sbuf", [128, NCOL * (D + 1)], "uint8"),
    "acc": ("psum", [128, 2 * BANK], "float32"),
    "yb": ("sbuf", [128, NCOL], "float32"),
}
SEMAPHORES = (["xin0", "xin1", "win", "xq0", "xq1", "wqd", "sent", "mm0", "mm1", "out0", "out1", "done0", "done1"]
              + ["a%d_%d" % (j, p) for j in range(N) for p in range(len(PIECES))])

_PLANS = {}


def _bits(mask):
    return [b for b in range(mask.bit_length()) if (mask >> b) & 1]


def _mask(bits):
    m = 0
    for b in bits:
        m |= 1 << b
    return m


def _plan(cores, src, topo):
    if "p" in _PLANS:
        return _PLANS["p"]
    n = len(cores)

    def way(a, b):
        if not topo.may_write(a, b):
            return None
        if topo.host(a) == topo.host(b) and topo.chip(a) == topo.chip(b):
            return "chip"
        return "switch" if topo.same_plane(a, b) else "cable"

    def helper(c):
        near = [k for k in range(max(0, c - 16), c + 16) if topo.host(k) == topo.host(c)]
        mate = [k for k in near if topo.mates(c, k)][0]
        return [k for k in near if way(c, k) == "chip" and k != c and k not in cores and topo.die(k) == topo.die(c)
                and topo.may_write(k, mate) != topo.may_write(c, mate)][0]

    first = {c: [] for c in cores}
    beside = {c: [] for c in cores}
    onward = {c: [] for c in cores}
    for j in range(n):
        o = cores[j]
        hosts = {}
        for r in range(n):
            if r != j and j in src[r]:
                hosts.setdefault(topo.host(cores[r]), []).append(cores[r])
        got, far = [], []
        for rs in hosts.values():
            k = way(o, rs[0])
            if k == "chip":
                beside[o] += [(j, r) for r in rs]
            elif k is None:
                far += rs
            else:
                p = ([r for r in rs if topo.die(r) == topo.die(o)] or rs)[0]
                first[o].append((j, p))
                got.append(p)
                onward[p] += [(j, r) for r in rs if r != p]
        for r in far:
            onward[[h for h in got if way(h, r) == "switch"][0]].append((j, r))

    calls = {c: [] for c in cores}
    due = {c: {} for c in cores}

    def engines(c, writes):
        far_mask = 0
        for o in cores:
            if way(c, o) not in (None, "chip"):
                far_mask |= topo.mask(c, o)
        low = _bits(far_mask)
        lows = [d for (_, d) in writes if way(c, d) != "chip"]
        out = []
        for (j, d) in writes:
            if way(c, d) == "chip":
                e = _bits(topo.mask(c, d) & ~far_mask)[0::2]
            elif len(lows) == 1:
                e = low
            else:
                e = low[lows.index(d)::2]
            out.append((j, d, e))
        return out

    def add(c, call, stage):
        if call:
            calls.setdefault(c, []).append(call)
            for (j, p, d, e) in call:
                due.setdefault(d, {}).setdefault(j, {})[p] = (stage, len(e))

    def together(c, ws, stage):
        add(c, [(j, p, d, e[p * len(e) // 2:(p + 1) * len(e) // 2]) for (j, d, e) in ws for p in range(2)], stage)
        add(c, [(j, PLANE, d, e) for (j, d, e) in ws], stage)

    for c in cores:
        ws = engines(c, first[c])
        cab = [w for w in ws if way(c, w[1]) == "cable"]
        oth = [w for w in ws if way(c, w[1]) != "cable"]
        h = helper(c)
        add(c, [(j, OWN[0], d, e) for (j, d, e) in cab], 2)
        add(c, [(j, FEED, hh, e) for (j, hh, e) in engines(c, [(j, h) for (j, _, _) in cab])], 2)
        for k, p in enumerate(OWN[1:3]):
            add(c, [(j, p, d, e) for (j, d, e) in cab], 2.1 + k / 10)
        together(c, oth, 2.3)
        for k, p in enumerate(OWN[3:]):
            add(c, [(j, p, d, e) for (j, d, e) in cab], 2.4 + k / 5)
        for k, p in enumerate(HELP):
            add(h, [(j, p, d, _bits(topo.mask(h, d))[0::2]) for (j, d, _) in cab], 2.5 + k / 5)
        together(c, engines(c, beside[c]), 3)
    for c in cores:
        slow = engines(c, [(j, d) for (j, d) in onward[c] if way(cores[j], c) == "cable"])
        for k, p in enumerate(TURN):
            add(c, [(j, p, d, e) for (j, d, e) in slow], 4 + k / len(TURN))
            if k == 1:
                together(c, engines(c, [(j, d) for (j, d) in onward[c] if way(cores[j], c) != "cable"]), 4.3)
    _PLANS["p"] = (calls, due)
    return _PLANS["p"]


def rank_program(g, core, T, topo):
    src = T.tables["SRC"]
    calls, due = _plan(T.cores, src, topo)
    if core not in calls:
        return
    rank = T.rank_of(core)
    S = T.sem

    def cols(c, j, p):
        r = T.rank_of(c)
        a = NCOL * (src[r].index(j) if r is not None and j in src[r] else D)
        return a + PIECES[p][0], a + PIECES[p][1]

    def covers(p, h):
        return PIECES[p][0] < HCOL * (h + 1) and PIECES[p][1] > HCOL * h

    def wait_for(queue, j, p):
        if j == rank:
            for h in range(2):
                if covers(p, h):
                    queue.wait_ge(S["xq%d" % h], 1)
        elif p in due[core][j]:
            queue.wait_ge(S["a%d_%d" % (j, p)], due[core][j][p][1])
        else:
            for k in sorted(due[core][j]):
                if k != PLANE and PIECES[k][0] <= PIECES[p][0] and PIECES[p][1] <= PIECES[k][1]:
                    queue.wait_ge(S["a%d_%d" % (j, k)], due[core][j][k][1])

    def parts(j, h):
        if j == rank:
            return [h]
        return [p for p in sorted(due[core][j]) if p == PLANE or covers(p, h)]

    if rank is not None:
        for p in range(2):
            g.sync.dma_start(T.xb[:, 4 * HCOL * p:4 * HCOL * (p + 1)], T.x[:, 4 * HCOL * p:4 * HCOL * (p + 1)]).then_inc(S["xin%d" % p], 16)
        g.sync.dma_start(T.wb[:], T.w[:]).then_inc(S.win, 16)

        for p in range(2):
            a, b = cols(core, rank, p)
            g.vector.wait_ge(S["xin%d" % p], 16)
            g.vector.quantize_mx(T.q[:, a:b], T.s[:, a:b], T.xb[:, 4 * HCOL * p:4 * HCOL * (p + 1)]).then_inc(S["xq%d" % p], 1)
        g.vector.wait_ge(S.win, 16)
        for i in range(D):
            g.vector.quantize_mx(T.wq[:, WCOL * i:WCOL * (i + 1)], T.ws[:, WCOL * i:WCOL * (i + 1)],
                                 T.wb[:, 4 * WCOL * i:4 * WCOL * (i + 1)]).then_inc(S.wqd, 1)

    left = 0
    for call in calls[core]:
        for (j, p) in sorted({(j, p) for (j, p, _, _) in call}):
            wait_for(g, j, p)
        trs = []
        for (j, p, d, eng) in call:
            sa, sb = cols(core, j, p)
            da, db = cols(d, j, p)
            rid, pid = topo.addr(d, core)
            if p == PLANE:
                s_ap, d_ap = T.s[:, sa:sb], T.s[:, da:db]
            else:
                s_ap, d_ap = T.q[:, sa:sb].bitcast(dt.uint8), T.q[:, da:db].bitcast(dt.uint8)
            trs.append(RemoteDMATransfer(dst_ids=[DstId(rid=rid, pnc=pid)], dma_engine_mask=_mask(eng),
                                         remote_sem=S["a%d_%d" % (j, p)], src=s_ap, dst=d_ap))
            left += len(eng)
        g.remote_dma_fused(trs, local_sem=S.sent)

    if rank is not None:
        def when(t):
            return 0 if t[0] == rank else max(due[core][t[0]][p][0] for p in parts(*t))

        order = sorted(((j, h) for j in src[rank] for h in range(2)), key=lambda t: (when(t), t[1], t[0]))
        done = [0, 0]
        g.tensor.wait_ge(S.wqd, D)
        for (j, h) in order:
            for p in parts(j, h):
                wait_for(g.tensor, j, p)
            i = src[rank].index(j)
            a, b = cols(core, j, h)
            done[h] += 1
            mm = g.tensor.matmul_mx(T.acc[:, BANK * h:BANK * h + HCOL], T.wq[:, WCOL * i:WCOL * (i + 1)], T.ws[:, WCOL * i:WCOL * (i + 1)],
                                    T.q[:, a:b], T.s[:, a:b], done[h] == 1, done[h] == D)
            if done[h] == D:
                mm.then_inc(S["mm%d" % h], 1)

        for p, queue in enumerate((g.sync, g.scalar)):
            g.vector.wait_ge(S["mm%d" % p], 1)
            g.vector.tensor_copy(T.yb[:, HCOL * p:HCOL * (p + 1)], T.acc[:, BANK * p:BANK * p + HCOL]).then_inc(S["out%d" % p], 1)
            queue.wait_ge(S["out%d" % p], 1)
            queue.dma_start(T.y[:, HCOL * p:HCOL * (p + 1)], T.yb[:, HCOL * p:HCOL * (p + 1)]).then_inc(S["done%d" % p], 16)
            queue.wait_ge(S["done%d" % p], 16)
    g.wait_ge(S.sent, left)
